import numpy as np
import ml_dtypes


def mxq(x, axis, fmt="e4m3"):
    dtype, down = {"e4m3": (ml_dtypes.float8_e4m3fn, 7), "e5m2": (ml_dtypes.float8_e5m2, 14)}[fmt]
    v = np.moveaxis(np.asarray(x, np.float32).astype(ml_dtypes.bfloat16).astype(np.float64), axis, -1)
    blocks = v.reshape(v.shape[:-1] + (-1, 32))
    amax = np.abs(blocks).max(-1, keepdims=True)
    byte = np.maximum(np.where(amax > 0, np.frexp(amax)[1] - 1 + 127, 0) - down, 1)
    scale = np.exp2(byte - 127.0)
    codes = (blocks / scale).astype(np.float32).astype(dtype).astype(np.float64)
    return np.moveaxis((codes * scale).reshape(v.shape), -1, axis)


WIDE = False


def mx_kscale(k):
    if not WIDE:
        return np.ones(k)
    levels = np.array([10, -10, 5, -5, 0])
    if k % 512:
        return np.exp2(np.random.permutation(np.resize(levels, k // 32))).repeat(32)
    a = np.empty((k // 512, 16))
    for p in range(k // 512):
        a[p, :8] = np.random.permutation(np.resize(levels, 8))
        for g in range(8):
            far = levels[np.abs(levels - a[p, g]) >= 10]
            a[p, g + 8] = far[np.random.randint(len(far))]
    return np.exp2(a.ravel()).repeat(32)


def f64(x):
    return np.asarray(x).astype(np.float64)


def striped8(idx):
    return np.asarray(idx).reshape(8, -1, 16).transpose(0, 2, 1).reshape(128, -1).astype(np.uint16)


def unstriped8(offs):
    return offs.reshape(8, 16, -1).transpose(0, 2, 1).reshape(8, -1).astype(np.int64)


def pick8(x, idx, run):
    r = np.arange(len(x))
    return x[r[:, None], idx[r % (8 * run) // run]]


E2M1 = np.array([0.0, 0.5, 1.0, 1.5, 2.0, 3.0, 4.0, 6.0, -0.0, -0.5, -1.0, -1.5, -2.0, -3.0, -4.0, -6.0])


def pack_weight(w, fmt):
    k, n = w.shape
    w = f64(np.asarray(w, np.float32).astype(ml_dtypes.bfloat16)).reshape(k // 32, 32, n)
    amax = np.abs(w).max(1)
    if fmt == "e4m3":
        byte = np.frexp(amax)[1] - 1 + 127 - 7
    else:
        mant, ex = np.frexp(amax / 6.0)
        byte = np.where(mant > 0.5, ex, ex - 1) + 127
    byte = np.clip(np.where(amax > 0, byte, 1), 1, 254)
    scaled = (w * np.exp2(127.0 - byte)[:, None, :]).reshape(k, n).astype(np.float32)
    by_word = np.ascontiguousarray(scaled.reshape(k // 512, 128, 4, n).transpose(0, 1, 3, 2))
    if fmt == "e4m3":
        words = by_word.astype(ml_dtypes.float8_e4m3fn).view(np.uint8)
    else:
        c = by_word.astype(ml_dtypes.float4_e2m1fn).view(np.uint8) & 0xF
        words = (c[..., 0::2] | (c[..., 1::2] << 4)).reshape(k // 512, 128, 2 * n)
    return np.ascontiguousarray(words), np.ascontiguousarray(byte.astype(np.uint8).reshape(k // 512, 16, n))


def unpack_weight(words, scales, fmt):
    g, _, n = scales.shape
    words = np.ascontiguousarray(words).reshape(g, 128, n, -1)
    if fmt == "e4m3":
        vals = words.view(ml_dtypes.float8_e4m3fn).astype(np.float64)
    else:
        nib = np.empty((g, 128, n, 4), np.uint8)
        nib[..., 0::2] = words & 0xF
        nib[..., 1::2] = words >> 4
        vals = E2M1[nib]
    vals = vals * np.repeat(np.exp2(scales.astype(np.float64) - 127.0), 8, axis=1)[..., None]
    return vals.transpose(0, 1, 3, 2).reshape(g * 512, n)


def sigmoid(v):
    return 1.0 / (1.0 + np.exp(-v))


D, T, I, Q = 512, 1024, 512, 128


def setup_inputs():
    n = np.random.standard_normal
    idx = np.stack([np.random.permutation(T)[:I] for _ in range(8)])
    idx2 = np.stack([np.random.permutation(T)[:I] for _ in range(8)])
    idx3 = np.stack([np.random.permutation(T)[:I] for _ in range(8)])
    idx4 = np.stack([np.random.permutation(T)[:I] for _ in range(8)])
    fd = mx_kscale(D)
    keysp = pack_weight(n((D, T)) / fd[:, None], "e4m3")
    tagsp = pack_weight(n((D, T)) / fd[:, None], "e2m1")
    return {
        "query": (n((D, Q)) * 0.75 / np.sqrt(D) * fd[:, None]).astype(np.float32),
        "query2": (n((D, Q)) * 0.75 / np.sqrt(D) * fd[:, None]).astype(np.float32),
        "keys_words": keysp[0],
        "keys_scales": keysp[1],
        "tags_words": tagsp[0],
        "tags_scales": tagsp[1],
        "thr": (np.random.uniform(-0.6, 0.6, (Q, 1))).astype(np.float32),
        "slope": (np.random.uniform(1.0, 3.0, (Q, 1))).astype(np.float32),
        "offs": striped8(idx),
        "offs2": striped8(idx2),
        "offs3": striped8(idx3),
        "offs4": striped8(idx4),
    }


def reference(query, query2, keys_words, keys_scales, tags_words, tags_scales, thr, slope, offs, offs2, offs3, offs4):
    idx = unstriped8(offs)
    idx2 = unstriped8(offs2)
    idx3 = unstriped8(offs3)
    idx4 = unstriped8(offs4)
    keysu = unpack_weight(keys_words, keys_scales, "e4m3")
    tagsu = unpack_weight(tags_words, tags_scales, "e2m1")
    queryq = mxq(f64(query), 0, "e4m3")
    query2q = mxq(f64(query2), 0, "e4m3")
    a = queryq.T @ keysu + query2q.T @ tagsu
    s1 = sigmoid(pick8(a, idx, 16) * f64(slope) + f64(thr))
    w = pick8(a, idx3, 16) * s1
    f1 = np.zeros((Q, T))
    f1[np.arange(Q)[:, None], idx2[np.arange(Q) % 128 // 16]] = w
    cc = a + f1
    y = pick8(cc, idx4, 16)
    return y

@@ -1,0 +1,122 @@
+from contextlib import ExitStack
+
+import concourse.mybir as mybir
+
+D, T, I, Q = 512, 1024, 512, 128
+FLOPS = 2 * 2 * D * Q * T
+
+F32 = mybir.dt.float32
+BF16 = mybir.dt.bfloat16
+I32 = mybir.dt.int32
+U32 = mybir.dt.uint32
+U16 = mybir.dt.uint16
+U8 = mybir.dt.uint8
+FP8X4 = mybir.dt.float8_e4m3fn_x4
+FP4X4 = mybir.dt.float4_e2m1fn_x4
+MULT = mybir.AluOpType.mult
+ADD = mybir.AluOpType.add
+SIGMOID = mybir.ActivationFunctionType.Sigmoid
+COPY = mybir.ActivationFunctionType.Copy
+
+P = 128
+PACK = 4
+BANK = 512
+HALF = I // 2
+LIST_HALF = HALF // 16
+KEY_ROW = 4
+
+
+def tile_attend_gatedhop_parts_kernel(tc, query, query2, keys_words, keys_scales, tags_words, tags_scales,
+                                       thr, slope, offs, offs2, offs3, offs4, out):
+    nc = tc.nc
+    with ExitStack() as ctx:
+        sb = ctx.enter_context(tc.tile_pool(name="sb", bufs=1))
+        ps = ctx.enter_context(tc.psum_pool(name="ps", bufs=1))
+
+        tag_plane = sb.tile([P, T], U8, name="tag_plane", align_bytes=64)
+        key_plane = sb.tile([P, T], U8, name="key_plane", align_bytes=64)
+        f1 = sb.tile([P, T], F32, name="f1")
+        nc.vector.memset(tag_plane[:].bitcast(I32), 0)
+        nc.vector.memset(key_plane[:].bitcast(I32), 0)
+        nc.vector.memset(f1[:], 0.0)
+
+        def load_plane(plane, scales, first_row):
+            rows = scales[0].rearrange("(q r) c -> r q c", r=PACK)
+            for r in range(PACK):
+                nc.scalar.dma_start(out=plane[first_row + r:P:32, :].bitcast(I32), in_=rows[r].bitcast(I32))
+
+        def load_query(src, name):
+            raw = sb.tile([P, PACK, Q], F32, name=name + "_raw")
+            nc.sync.dma_start(out=raw[:], in_=src.rearrange("(p j) w -> p j w", j=PACK))
+            return raw
+
+        def quantise(raw, name):
+            grouped = sb.tile([P, Q * PACK], BF16, name=name + "_bf", align_bytes=64)
+            nc.vector.tensor_copy(
+                out=grouped[:].rearrange("p (c i t) -> p c t i", i=4, t=PACK),
+                in_=raw[:].rearrange("p t (c i) -> p c t i", i=4))
+            codes = sb.tile([P, Q], U32, name=name + "_codes", align_bytes=64)
+            plane = sb.tile([P, Q], U8, name=name + "_plane", align_bytes=64)
+            nc.vector.quantize_mx(out=codes[:].bitcast(FP8X4), scales=plane[:], in_=grouped[:])
+            return codes, plane
+
+        load_plane(tag_plane, tags_scales, 0)
+        q2_raw = load_query(query2, "q2")
+        tags = sb.tile([P, 2 * T], U8, name="tags", align_bytes=64)
+        nc.sync.dma_start(out=tags[:].bitcast(I32), in_=tags_words[0].bitcast(I32))
+        q_raw = load_query(query, "q")
+        key_bytes = keys_words[0].rearrange("p n t -> p (n t)")
+        keys = []
+        for b in range(T // BANK):
+            half = sb.tile([P, BANK], I32, name="keys%d" % b, align_bytes=64)
+            nc.sync.dma_start(out=half[:], in_=key_bytes[:, PACK * BANK * b:PACK * BANK * (b + 1)].bitcast(I32))
+            keys.append(half)
+        load_plane(key_plane, keys_scales, KEY_ROW)
+
+        slope_t = sb.tile([P, 1], F32, name="slope_t")
+        thr_t = sb.tile([P, 1], F32, name="thr_t")
+        nc.gpsimd.dma_start(out=slope_t[:], in_=slope)
+        nc.gpsimd.dma_start(out=thr_t[:], in_=thr)
+
+        lists = []
+        for name, src in (("o1", offs), ("o3", offs3), ("o2", offs2), ("o4", offs4)):
+            t = sb.tile([P, I // 16], U16, name=name)
+            nc.sync.dma_start(t[:], src)
+            lists.append(t)
+        o1, o3, o2, o4 = lists
+
+        q2_codes, q2_plane = quantise(q2_raw, "q2")
+        q_codes, q_plane = quantise(q_raw, "q")
+
+        banks = [ps.tile([P, BANK], F32, name="bank%d" % b) for b in range(T // BANK)]
+        for b in range(T // BANK):
+            nc.tensor.matmul_mx(out=banks[b][:], lhsT=q2_codes[:].bitcast(FP8X4), lhsT_scale=q2_plane[:],
+                                rhs=tags[:, 2 * BANK * b:2 * BANK * (b + 1)].bitcast(FP4X4),
+                                rhs_scale=tag_plane[:, BANK * b:BANK * (b + 1)], start=True, stop=False)
+        a = sb.tile([P, T], F32, name="a")
+        for b in range(T // BANK):
+            nc.tensor.matmul_mx(out=banks[b][:], lhsT=q_codes[:].bitcast(FP8X4), lhsT_scale=q_plane[:],
+                                rhs=keys[b][:].bitcast(FP8X4),
+                                rhs_scale=key_plane[KEY_ROW:P, BANK * b:BANK * (b + 1)], start=False, stop=True)
+            nc.vector.tensor_copy(out=a[:, BANK * b:BANK * (b + 1)], in_=banks[b][:])
+
+        def piece(lst, h):
+            return lst[:, LIST_HALF * h:LIST_HALF * (h + 1)]
+
+        gate = [sb.tile([P, HALF], F32, name="gate%d" % h) for h in range(2)]
+        val = [sb.tile([P, HALF], F32, name="val%d" % h) for h in range(2)]
+        nc.scalar.activation(gate[0][:], a[:].indirect(piece(o1, 0)), SIGMOID, bias=thr_t[:], scale=slope_t[:])
+        nc.vector.tensor_copy(val[0][:], a[:].indirect(piece(o3, 0)))
+        nc.scalar.activation(gate[1][:], a[:].indirect(piece(o1, 1)), SIGMOID, bias=thr_t[:], scale=slope_t[:])
+        nc.scalar.activation(val[1][:], a[:].indirect(piece(o3, 1)), COPY)
+        for h in range(2):
+            nc.vector.tensor_tensor(f1[:].indirect(piece(o2, h)), val[h][:], gate[h][:], MULT)
+
+        cc = sb.tile([P, T], F32, name="cc")
+        nc.vector.tensor_tensor(cc[:], a[:], f1[:], ADD)
+
+        res = [sb.tile([P, HALF], F32, name="res%d" % h) for h in range(2)]
+        nc.vector.tensor_copy(res[0][:], cc[:].indirect(piece(o4, 0)))
+        nc.sync.dma_start(out=out[:, 0:HALF], in_=res[0][:])
+        nc.scalar.activation(res[1][:], cc[:].indirect(piece(o4, 1)), COPY)
+        nc.scalar.dma_start(out=out[:, HALF:I], in_=res[1][:])

@@ -40,10 +40,15 @@ def tile_attend_gatedhop_parts_kernel(tc, query, query2, keys_words, keys_scales
         nc.vector.memset(key_plane[:].bitcast(I32), 0)
         nc.vector.memset(f1[:], 0.0)
 
+        warm_in = sb.tile([P, 1], F32, name="warm_in")
+        warm_out = sb.tile([P, 1], F32, name="warm_out")
+        nc.vector.memset(warm_in[:], 0.0)
+        nc.scalar.activation(warm_out[:], warm_in[:], SIGMOID)
+
         def load_plane(plane, scales, first_row):
             rows = scales[0].rearrange("(q r) c -> r q c", r=PACK)
             for r in range(PACK):
-                nc.scalar.dma_start(out=plane[first_row + r:P:32, :].bitcast(I32), in_=rows[r].bitcast(I32))
+                nc.sync.dma_start(out=plane[first_row + r:P:32, :].bitcast(I32), in_=rows[r].bitcast(I32))
 
         def load_query(src, name):
             raw = sb.tile([P, PACK, Q], F32, name=name + "_raw")
@@ -51,17 +56,21 @@ def tile_attend_gatedhop_parts_kernel(tc, query, query2, keys_words, keys_scales
             return raw
 
         def quantise(raw, name):
-            grouped = sb.tile([P, Q * PACK], BF16, name=name + "_bf", align_bytes=64)
-            nc.vector.tensor_copy(
-                out=grouped[:].rearrange("p (c i t) -> p c t i", i=4, t=PACK),
-                in_=raw[:].rearrange("p t (c i) -> p c t i", i=4))
             codes = sb.tile([P, Q], U32, name=name + "_codes", align_bytes=64)
             plane = sb.tile([P, Q], U8, name=name + "_plane", align_bytes=64)
-            nc.vector.quantize_mx(out=codes[:].bitcast(FP8X4), scales=plane[:], in_=grouped[:])
+            halves = []
+            for h, cast in enumerate((nc.vector.tensor_copy, nc.scalar.copy)):
+                cols = slice(h * Q // 2, (h + 1) * Q // 2)
+                grouped = sb.tile([P, Q // 2 * PACK], BF16, name=name + "_bf%d" % h, align_bytes=64)
+                cast(grouped[:].rearrange("p (c i t) -> p c t i", i=4, t=PACK),
+                     raw[:, :, cols].rearrange("p t (c i) -> p c t i", i=4))
+                halves.append((cols, grouped))
+            for cols, grouped in reversed(halves):
+                nc.vector.quantize_mx(out=codes[:, cols].bitcast(FP8X4), scales=plane[:, cols], in_=grouped[:])
             return codes, plane
 
-        load_plane(tag_plane, tags_scales, 0)
         q2_raw = load_query(query2, "q2")
+        load_plane(tag_plane, tags_scales, 0)
         tags = sb.tile([P, 2 * T], U8, name="tags", align_bytes=64)
         nc.sync.dma_start(out=tags[:].bitcast(I32), in_=tags_words[0].bitcast(I32))
         q_raw = load_query(query, "q")
@@ -71,7 +80,8 @@ def tile_attend_gatedhop_parts_kernel(tc, query, query2, keys_words, keys_scales
             half = sb.tile([P, BANK], I32, name="keys%d" % b, align_bytes=64)
             nc.sync.dma_start(out=half[:], in_=key_bytes[:, PACK * BANK * b:PACK * BANK * (b + 1)].bitcast(I32))
             keys.append(half)
-        load_plane(key_plane, keys_scales, KEY_ROW)
+            if b == 0:
+                load_plane(key_plane, keys_scales, KEY_ROW)
 
         slope_t = sb.tile([P, 1], F32, name="slope_t")
         thr_t = sb.tile([P, 1], F32, name="thr_t")
@@ -88,17 +98,22 @@ def tile_attend_gatedhop_parts_kernel(tc, query, query2, keys_words, keys_scales
         q2_codes, q2_plane = quantise(q2_raw, "q2")
         q_codes, q_plane = quantise(q_raw, "q")
 
-        banks = [ps.tile([P, BANK], F32, name="bank%d" % b) for b in range(T // BANK)]
-        for b in range(T // BANK):
-            nc.tensor.matmul_mx(out=banks[b][:], lhsT=q2_codes[:].bitcast(FP8X4), lhsT_scale=q2_plane[:],
-                                rhs=tags[:, 2 * BANK * b:2 * BANK * (b + 1)].bitcast(FP4X4),
-                                rhs_scale=tag_plane[:, BANK * b:BANK * (b + 1)], start=True, stop=False)
+        spans = [(lo, lo + 256) for lo in range(0, T, 256)]
+        banks = [ps.tile([P, hi - lo], F32, name="bank%d" % lo) for lo, hi in spans]
+        for bank, (lo, hi) in zip(banks, spans):
+            nc.tensor.matmul_mx(out=bank[:], lhsT=q2_codes[:].bitcast(FP8X4), lhsT_scale=q2_plane[:],
+                                rhs=tags[:, 2 * lo:2 * hi].bitcast(FP4X4),
+                                rhs_scale=tag_plane[:, lo:hi], start=True, stop=False)
         a = sb.tile([P, T], F32, name="a")
-        for b in range(T // BANK):
-            nc.tensor.matmul_mx(out=banks[b][:], lhsT=q_codes[:].bitcast(FP8X4), lhsT_scale=q_plane[:],
-                                rhs=keys[b][:].bitcast(FP8X4),
-                                rhs_scale=key_plane[KEY_ROW:P, BANK * b:BANK * (b + 1)], start=False, stop=True)
-            nc.vector.tensor_copy(out=a[:, BANK * b:BANK * (b + 1)], in_=banks[b][:])
+        for bank, (lo, hi) in zip(banks, spans):
+            b = lo // BANK
+            nc.tensor.matmul_mx(out=bank[:], lhsT=q_codes[:].bitcast(FP8X4), lhsT_scale=q_plane[:],
+                                rhs=keys[b][:, lo - b * BANK:hi - b * BANK].bitcast(FP8X4),
+                                rhs_scale=key_plane[KEY_ROW:P, lo:hi], start=False, stop=True)
+            if lo % BANK == 0:
+                nc.scalar.copy(a[:, lo:hi], bank[:])
+            else:
+                nc.vector.tensor_copy(out=a[:, lo:hi], in_=bank[:])
 
         def piece(lst, h):
             return lst[:, LIST_HALF * h:LIST_HALF * (h + 1)]

@@ -24,6 +24,8 @@ BANK = 512
 HALF = I // 2
 LIST_HALF = HALF // 16
 KEY_ROW = 4
+KEYS_FIRST = 512
+ADD_SPLIT = 640
 
 
 def tile_attend_gatedhop_parts_kernel(tc, query, query2, keys_words, keys_scales, tags_words, tags_scales,
@@ -76,11 +78,11 @@ def tile_attend_gatedhop_parts_kernel(tc, query, query2, keys_words, keys_scales
         q_raw = load_query(query, "q")
         key_bytes = keys_words[0].rearrange("p n t -> p (n t)")
         keys = []
-        for b in range(T // BANK):
-            half = sb.tile([P, BANK], I32, name="keys%d" % b, align_bytes=64)
-            nc.sync.dma_start(out=half[:], in_=key_bytes[:, PACK * BANK * b:PACK * BANK * (b + 1)].bitcast(I32))
-            keys.append(half)
-            if b == 0:
+        for lo, hi in ((0, KEYS_FIRST), (KEYS_FIRST, T)):
+            part = sb.tile([P, hi - lo], I32, name="keys%d" % lo, align_bytes=64)
+            nc.sync.dma_start(out=part[:], in_=key_bytes[:, PACK * lo:PACK * hi].bitcast(I32))
+            keys.append(part)
+            if lo == 0:
                 load_plane(key_plane, keys_scales, KEY_ROW)
 
         slope_t = sb.tile([P, 1], F32, name="slope_t")
@@ -106,11 +108,11 @@ def tile_attend_gatedhop_parts_kernel(tc, query, query2, keys_words, keys_scales
                                 rhs_scale=tag_plane[:, lo:hi], start=True, stop=False)
         a = sb.tile([P, T], F32, name="a")
         for bank, (lo, hi) in zip(banks, spans):
-            b = lo // BANK
+            part, first = (keys[0], 0) if lo < KEYS_FIRST else (keys[1], KEYS_FIRST)
             nc.tensor.matmul_mx(out=bank[:], lhsT=q_codes[:].bitcast(FP8X4), lhsT_scale=q_plane[:],
-                                rhs=keys[b][:, lo - b * BANK:hi - b * BANK].bitcast(FP8X4),
+                                rhs=part[:, lo - first:hi - first].bitcast(FP8X4),
                                 rhs_scale=key_plane[KEY_ROW:P, lo:hi], start=False, stop=True)
-            if lo % BANK == 0:
+            if lo % BANK != 0:
                 nc.scalar.copy(a[:, lo:hi], bank[:])
             else:
                 nc.vector.tensor_copy(out=a[:, lo:hi], in_=bank[:])
@@ -128,7 +130,11 @@ def tile_attend_gatedhop_parts_kernel(tc, query, query2, keys_words, keys_scales
             nc.vector.tensor_tensor(f1[:].indirect(piece(o2, h)), val[h][:], gate[h][:], MULT)
 
         cc = sb.tile([P, T], F32, name="cc")
-        nc.vector.tensor_tensor(cc[:], a[:], f1[:], ADD)
+        for bank, (lo, hi) in zip(banks, spans):
+            end = min(hi, ADD_SPLIT)
+            if end > lo:
+                nc.vector.tensor_tensor(cc[:, lo:end], bank[:, 0:end - lo], f1[:, lo:end], ADD)
+        nc.gpsimd.tensor_tensor(cc[:, ADD_SPLIT:T], a[:, ADD_SPLIT:T], f1[:, ADD_SPLIT:T], ADD)
 
         res = [sb.tile([P, HALF], F32, name="res%d" % h) for h in range(2)]
         nc.vector.tensor_copy(res[0][:], cc[:].indirect(piece(o4, 0)))

@@ -42,28 +42,24 @@ def tile_attend_gatedhop_parts_kernel(tc, query, query2, keys_words, keys_scales
         nc.vector.memset(key_plane[:].bitcast(I32), 0)
         nc.vector.memset(f1[:], 0.0)
 
-        warm_in = sb.tile([P, 1], F32, name="warm_in")
-        warm_out = sb.tile([P, 1], F32, name="warm_out")
-        nc.vector.memset(warm_in[:], 0.0)
-        nc.scalar.activation(warm_out[:], warm_in[:], SIGMOID)
-
-        def load_plane(plane, scales, first_row):
+        def load_plane(plane, scales, first_row, queues):
             rows = scales[0].rearrange("(q r) c -> r q c", r=PACK)
             for r in range(PACK):
-                nc.sync.dma_start(out=plane[first_row + r:P:32, :].bitcast(I32), in_=rows[r].bitcast(I32))
+                queues[r].dma_start(out=plane[first_row + r:P:32, :].bitcast(I32), in_=rows[r].bitcast(I32))
 
         def load_query(src, name):
             raw = sb.tile([P, PACK, Q], F32, name=name + "_raw")
             nc.sync.dma_start(out=raw[:], in_=src.rearrange("(p j) w -> p j w", j=PACK))
             return raw
 
-        def quantise(raw, name):
+        def quantise(raw, name, casts):
             codes = sb.tile([P, Q], U32, name=name + "_codes", align_bytes=64)
             plane = sb.tile([P, Q], U8, name=name + "_plane", align_bytes=64)
             halves = []
-            for h, cast in enumerate((nc.vector.tensor_copy, nc.scalar.copy)):
-                cols = slice(h * Q // 2, (h + 1) * Q // 2)
-                grouped = sb.tile([P, Q // 2 * PACK], BF16, name=name + "_bf%d" % h, align_bytes=64)
+            for h, cast in enumerate(casts):
+                width = Q // len(casts)
+                cols = slice(h * width, (h + 1) * width)
+                grouped = sb.tile([P, width * PACK], BF16, name=name + "_bf%d" % h, align_bytes=64)
                 cast(grouped[:].rearrange("p (c i t) -> p c t i", i=4, t=PACK),
                      raw[:, :, cols].rearrange("p t (c i) -> p c t i", i=4))
                 halves.append((cols, grouped))
@@ -72,7 +68,12 @@ def tile_attend_gatedhop_parts_kernel(tc, query, query2, keys_words, keys_scales
             return codes, plane
 
         q2_raw = load_query(query2, "q2")
-        load_plane(tag_plane, tags_scales, 0)
+        load_plane(tag_plane, tags_scales, 0, (nc.sync, nc.scalar, nc.sync, nc.scalar))
+        warm_in = sb.tile([P, 1], F32, name="warm_in")
+        warm_out = sb.tile([P, 1], F32, name="warm_out")
+        nc.vector.memset(warm_in[:], 0.0)
+        nc.scalar.activation(warm_out[:], warm_in[:], SIGMOID)
+
         tags = sb.tile([P, 2 * T], U8, name="tags", align_bytes=64)
         nc.sync.dma_start(out=tags[:].bitcast(I32), in_=tags_words[0].bitcast(I32))
         q_raw = load_query(query, "q")
@@ -83,7 +84,7 @@ def tile_attend_gatedhop_parts_kernel(tc, query, query2, keys_words, keys_scales
             nc.sync.dma_start(out=part[:], in_=key_bytes[:, PACK * lo:PACK * hi].bitcast(I32))
             keys.append(part)
             if lo == 0:
-                load_plane(key_plane, keys_scales, KEY_ROW)
+                load_plane(key_plane, keys_scales, KEY_ROW, (nc.sync,) * PACK)
 
         slope_t = sb.tile([P, 1], F32, name="slope_t")
         thr_t = sb.tile([P, 1], F32, name="thr_t")
@@ -97,10 +98,10 @@ def tile_attend_gatedhop_parts_kernel(tc, query, query2, keys_words, keys_scales
             lists.append(t)
         o1, o3, o2, o4 = lists
 
-        q2_codes, q2_plane = quantise(q2_raw, "q2")
-        q_codes, q_plane = quantise(q_raw, "q")
+        q2_codes, q2_plane = quantise(q2_raw, "q2", (nc.vector.tensor_copy,))
+        q_codes, q_plane = quantise(q_raw, "q", (nc.vector.tensor_copy, nc.scalar.copy))
 
-        spans = [(lo, lo + 256) for lo in range(0, T, 256)]
+        spans = [(0, 256), (256, 512), (512, 768), (768, 896), (896, 1024)]
         banks = [ps.tile([P, hi - lo], F32, name="bank%d" % lo) for lo, hi in spans]
         for bank, (lo, hi) in zip(banks, spans):
             nc.tensor.matmul_mx(out=bank[:], lhsT=q2_codes[:].bitcast(FP8X4), lhsT_scale=q2_plane[:],

from contextlib import ExitStack

import concourse.mybir as mybir

D, T, I, Q = 512, 1024, 512, 128
FLOPS = 2 * 2 * D * Q * T

F32 = mybir.dt.float32
BF16 = mybir.dt.bfloat16
I32 = mybir.dt.int32
U32 = mybir.dt.uint32
U16 = mybir.dt.uint16
U8 = mybir.dt.uint8
FP8X4 = mybir.dt.float8_e4m3fn_x4
FP4X4 = mybir.dt.float4_e2m1fn_x4
MULT = mybir.AluOpType.mult
ADD = mybir.AluOpType.add
SIGMOID = mybir.ActivationFunctionType.Sigmoid
COPY = mybir.ActivationFunctionType.Copy

P = 128
PACK = 4
BANK = 512
HALF = I // 2
LIST_HALF = HALF // 16
KEY_ROW = 4
KEYS_FIRST = 512
ADD_SPLIT = 640


def tile_attend_gatedhop_parts_kernel(tc, query, query2, keys_words, keys_scales, tags_words, tags_scales,
                                       thr, slope, offs, offs2, offs3, offs4, out):
    nc = tc.nc
    with ExitStack() as ctx:
        sb = ctx.enter_context(tc.tile_pool(name="sb", bufs=1))
        ps = ctx.enter_context(tc.psum_pool(name="ps", bufs=1))

        tag_plane = sb.tile([P, T], U8, name="tag_plane", align_bytes=64)
        key_plane = sb.tile([P, T], U8, name="key_plane", align_bytes=64)
        f1 = sb.tile([P, T], F32, name="f1")
        nc.vector.memset(tag_plane[:].bitcast(I32), 0)
        nc.vector.memset(key_plane[:].bitcast(I32), 0)
        nc.vector.memset(f1[:], 0.0)

        def load_plane(plane, scales, first_row, queues):
            rows = scales[0].rearrange("(q r) c -> r q c", r=PACK)
            for r in range(PACK):
                queues[r].dma_start(out=plane[first_row + r:P:32, :].bitcast(I32), in_=rows[r].bitcast(I32))

        def load_query(src, name):
            raw = sb.tile([P, PACK, Q], F32, name=name + "_raw")
            nc.sync.dma_start(out=raw[:], in_=src.rearrange("(p j) w -> p j w", j=PACK))
            return raw

        def quantise(raw, name, casts):
            codes = sb.tile([P, Q], U32, name=name + "_codes", align_bytes=64)
            plane = sb.tile([P, Q], U8, name=name + "_plane", align_bytes=64)
            halves = []
            for h, cast in enumerate(casts):
                width = Q // len(casts)
                cols = slice(h * width, (h + 1) * width)
                grouped = sb.tile([P, width * PACK], BF16, name=name + "_bf%d" % h, align_bytes=64)
                cast(grouped[:].rearrange("p (c i t) -> p c t i", i=4, t=PACK),
                     raw[:, :, cols].rearrange("p t (c i) -> p c t i", i=4))
                halves.append((cols, grouped))
            for cols, grouped in reversed(halves):
                nc.vector.quantize_mx(out=codes[:, cols].bitcast(FP8X4), scales=plane[:, cols], in_=grouped[:])
            return codes, plane

        q2_raw = load_query(query2, "q2")
        load_plane(tag_plane, tags_scales, 0, (nc.sync, nc.scalar, nc.sync, nc.scalar))
        warm_in = sb.tile([P, 1], F32, name="warm_in")
        warm_out = sb.tile([P, 1], F32, name="warm_out")
        nc.vector.memset(warm_in[:], 0.0)
        nc.scalar.activation(warm_out[:], warm_in[:], SIGMOID)

        tags = sb.tile([P, 2 * T], U8, name="tags", align_bytes=64)
        nc.sync.dma_start(out=tags[:].bitcast(I32), in_=tags_words[0].bitcast(I32))
        q_raw = load_query(query, "q")
        key_bytes = keys_words[0].rearrange("p n t -> p (n t)")
        keys = []
        for lo, hi in ((0, KEYS_FIRST), (KEYS_FIRST, T)):
            part = sb.tile([P, hi - lo], I32, name="keys%d" % lo, align_bytes=64)
            nc.sync.dma_start(out=part[:], in_=key_bytes[:, PACK * lo:PACK * hi].bitcast(I32))
            keys.append(part)
            if lo == 0:
                load_plane(key_plane, keys_scales, KEY_ROW, (nc.sync,) * PACK)

        slope_t = sb.tile([P, 1], F32, name="slope_t")
        thr_t = sb.tile([P, 1], F32, name="thr_t")
        nc.gpsimd.dma_start(out=slope_t[:], in_=slope)
        nc.gpsimd.dma_start(out=thr_t[:], in_=thr)

        lists = []
        for name, src in (("o1", offs), ("o3", offs3), ("o2", offs2), ("o4", offs4)):
            t = sb.tile([P, I // 16], U16, name=name)
            nc.sync.dma_start(t[:], src)
            lists.append(t)
        o1, o3, o2, o4 = lists

        q2_codes, q2_plane = quantise(q2_raw, "q2", (nc.vector.tensor_copy,))
        q_codes, q_plane = quantise(q_raw, "q", (nc.vector.tensor_copy, nc.scalar.copy))

        spans = [(0, 256), (256, 512), (512, 768), (768, 896), (896, 1024)]
        banks = [ps.tile([P, hi - lo], F32, name="bank%d" % lo) for lo, hi in spans]
        for bank, (lo, hi) in zip(banks, spans):
            nc.tensor.matmul_mx(out=bank[:], lhsT=q2_codes[:].bitcast(FP8X4), lhsT_scale=q2_plane[:],
                                rhs=tags[:, 2 * lo:2 * hi].bitcast(FP4X4),
                                rhs_scale=tag_plane[:, lo:hi], start=True, stop=False)
        a = sb.tile([P, T], F32, name="a")
        for bank, (lo, hi) in zip(banks, spans):
            part, first = (keys[0], 0) if lo < KEYS_FIRST else (keys[1], KEYS_FIRST)
            nc.tensor.matmul_mx(out=bank[:], lhsT=q_codes[:].bitcast(FP8X4), lhsT_scale=q_plane[:],
                                rhs=part[:, lo - first:hi - first].bitcast(FP8X4),
                                rhs_scale=key_plane[KEY_ROW:P, lo:hi], start=False, stop=True)
            if lo % BANK != 0:
                nc.scalar.copy(a[:, lo:hi], bank[:])
            else:
                nc.vector.tensor_copy(out=a[:, lo:hi], in_=bank[:])

        def piece(lst, h):
            return lst[:, LIST_HALF * h:LIST_HALF * (h + 1)]

        gate = [sb.tile([P, HALF], F32, name="gate%d" % h) for h in range(2)]
        val = [sb.tile([P, HALF], F32, name="val%d" % h) for h in range(2)]
        nc.scalar.activation(gate[0][:], a[:].indirect(piece(o1, 0)), SIGMOID, bias=thr_t[:], scale=slope_t[:])
        nc.vector.tensor_copy(val[0][:], a[:].indirect(piece(o3, 0)))
        nc.scalar.activation(gate[1][:], a[:].indirect(piece(o1, 1)), SIGMOID, bias=thr_t[:], scale=slope_t[:])
        nc.scalar.activation(val[1][:], a[:].indirect(piece(o3, 1)), COPY)
        for h in range(2):
            nc.vector.tensor_tensor(f1[:].indirect(piece(o2, h)), val[h][:], gate[h][:], MULT)

        cc = sb.tile([P, T], F32, name="cc")
        for bank, (lo, hi) in zip(banks, spans):
            end = min(hi, ADD_SPLIT)
            if end > lo:
                nc.vector.tensor_tensor(cc[:, lo:end], bank[:, 0:end - lo], f1[:, lo:end], ADD)
        nc.gpsimd.tensor_tensor(cc[:, ADD_SPLIT:T], a[:, ADD_SPLIT:T], f1[:, ADD_SPLIT:T], ADD)

        res = [sb.tile([P, HALF], F32, name="res%d" % h) for h in range(2)]
        nc.vector.tensor_copy(res[0][:], cc[:].indirect(piece(o4, 0)))
        nc.sync.dma_start(out=out[:, 0:HALF], in_=res[0][:])
        nc.scalar.activation(res[1][:], cc[:].indirect(piece(o4, 1)), COPY)
        nc.scalar.dma_start(out=out[:, HALF:I], in_=res[1][:])
